import numpy as np, ml_dtypes
CORES = [32,40,48,56,64,72,80,88,96,104,112,120]
N = 12
import mx_ref
NC, G = 128, 2
C = np.float32(0.023)
BF = ml_dtypes.bfloat16
def tile(rs):
    return np.stack(rs, axis=2).reshape(128, -1).astype(BF)
def act(Z):
    return [np.maximum(s * z, 0) * C for z in Z for s in (1, -1)]
def pk(c, s, i=0):
    return (np.ascontiguousarray(c[:, 512 * i:512 * i + 512]), mx_ref.live(s[:, 128 * i:128 * i + 128]))
def inputs(rng, e, E):
    def f(*shape):
        v = (rng.standard_normal(shape, dtype=np.float32) * np.exp2(rng.integers(-2, 3, shape[:-1] + (1,)))).astype(BF)
        return mx_ref.spread((v.astype(np.float32) * np.exp2(rng.integers(-E, E + 1, shape[:-2] + (1, 1))).astype(np.float32)).astype(BF), rng, e)
    def packed(k):
        c = np.zeros((N, 128, k * 512), np.uint8); s = np.zeros((N, 128, k * 128), np.uint8)
        for r in range(N):
            for i in range(k):
                a, b = mx_ref.quantize(f(128, 512)); c[r][:, 512 * i:512 * i + 512] = a; s[r][:, 128 * i:128 * i + 128] = mx_ref.plane(b, rng)
        return c, s
    d = {}
    d["ac"], d["az"] = packed(1)
    d["bc"], d["bs"] = packed(1)
    d["cc"], d["cs"] = packed(1)
    d["x"] = f(N, 128, 4 * NC)
    return d
def setup_inputs(rng):
    return inputs(rng, 0, 0)
def setup_inputs_blocks(rng):
    return inputs(rng, 2, 0)
def setup_inputs_wide(rng):
    return inputs(rng, 0, 4)
def reference(ac, az, bc, bs, cc, cs, x):
    y = np.zeros((N, 128, N * NC), np.float32)
    for r in range(N):
        h = mx_ref.quantize(tile(act([mx_ref.matmul(pk(ac[i], az[i]), mx_ref.quantize(x[r])) for i in range(G)])))
        h = mx_ref.quantize(tile(act([mx_ref.matmul(pk(bc[i], bs[i]), h) for i in range(G)])))
        for j in range(N):
            y[r][:, NC * j:NC * j + NC] = mx_ref.matmul(pk(cc[j], cs[j]), h)
    return {"y": y}

from concourse.bass import DstId, RemoteDMATransfer
from concourse.mybir import dt, AluOpType, ActivationFunctionType

N = 12
G = 2
W = 128
CW, CS = 2, 3
YS = 2
BANK = 512
SCALE = 0.023

CODES, PLANE = "float8_e4m3fn_x4", "uint8"
SCRATCH = {
    "a_w": ("sbuf", [128, W], CODES), "a_s": ("sbuf", [128, W], PLANE),
    "b_w": ("sbuf", [128, W], CODES), "b_s": ("sbuf", [128, G * W], PLANE),
    "c_w": ("sbuf", [128, CW * W], CODES), "c_s": ("sbuf", [128, CS * W], PLANE),
    "y_s": ("sbuf", [128, YS * W], "float32"),
    "zp": ("psum", [128, 2 * BANK], "float32"),
    "up": ("psum", [128, 2 * BANK], "float32"),
    "yp": ("psum", [128, 4 * BANK], "float32"),
}
for _t in "xgh":
    SCRATCH["t" + _t] = ("sbuf", [128, 4 * W], "bfloat16")
    SCRATCH["q%s_w" % _t] = ("sbuf", [128, W], CODES)
    SCRATCH["q%s_s" % _t] = ("sbuf", [128, W], PLANE)
for _t, _n in (("a", G), ("b", G), ("c", N)):
    for _j in range(_n):
        SCRATCH["%sd%d_w" % (_t, _j)] = ("dram", [128, W], CODES)
        SCRATCH["%sd%d_s" % (_t, _j)] = ("dram", [128, W], PLANE)

SEMAPHORES = ["sent", "ld_a", "ld_b", "ld_c", "x_in", "qx", "qg", "qh",
              "ha_w", "ha_s", "hb_w", "hb_s", "hc_w", "hc_s", "rsg", "rvg", "rsh", "rvh", "fbs"]
SEMAPHORES += ["%s%d" % (p, i) for p in ("a", "b", "z", "u", "fa", "fb") for i in range(G)]
SEMAPHORES += ["%s%d" % (p, i) for p in ("c", "fc", "fp", "mm", "cp", "st") for i in range(N)]


def _count(mask):
    return bin(mask).count("1")


def _common(topo, core, dsts):
    m = topo.mask(core, dsts[0])
    for d in dsts:
        m &= topo.mask(core, d)
    return m


def _plan(r, T, topo):
    core = T.cores[r]
    others = [T.cores[(r + k) % N] for k in range(1, N)]
    same = [d for d in others if topo.may_write(core, d)]
    cross = [d for d in others if not topo.may_write(core, d)]
    cross.sort(key=lambda d: not topo.mates(topo.chip(core), topo.chip(d)))
    ports = [c for c in range(128) if topo.chip(c) == topo.chip(core) and topo.may_write(c, cross[0])]
    near = [c for c in ports if topo.die(c) == topo.die(core)]
    far = [c for c in ports if topo.die(c) != topo.die(core)]
    three = [near[0], far[0], far[1]]
    ab = {c: cross[k::3] for k, c in enumerate(three)}
    cc = {c: cross[k::2] for k, c in enumerate(far)}
    return core, same, ab, cc


def rank_program(g, core, T, topo):
    sem = T.sem
    rank = T.rank_of(core)
    sent = [0]

    def cols(i):
        return slice(W * i, W * i + W)

    def codes(name):
        return T[name + "_w"][:].bitcast(dt.uint8)

    def plane(name):
        return T[name + "_s"][:]

    def send(view, dsts, mask, s):
        ids = []
        for d in dsts:
            rid, pid, _ = topo.addr(d)
            ids.append(DstId(rid=rid, pnc=pid))
        g.remote_dma_fused([RemoteDMATransfer(dst_ids=ids, dma_engine_mask=mask, remote_sem=sem[s],
                                              srcs=[view], dsts=[view] * len(dsts), alu_op=0)], local_sem=sem["sent"])
        sent[0] += _count(mask)

    def masks(r, owner, same, ab):
        on, off = _common(topo, owner, list(ab)), _common(topo, owner, same)
        return off, (on & ~off) if r < G else (on & off)

    if rank is None:
        for r in range(N):
            if topo.chip(T.cores[r]) == topo.chip(core):
                owner, same, ab, cc = _plan(r, T, topo)
                front = _count(masks(r, owner, same, ab)[1])
                jobs = []
                if r < G and core in ab:
                    jobs += [("ha", "ad%d" % r, ab[core], "a%d" % r), ("hb", "bd%d" % r, ab[core], "b%d" % r)]
                if core in cc:
                    jobs.append(("hc", "cd%d" % r, cc[core], "c%d" % r))
                for h, name, dsts, s in jobs:
                    m = _common(topo, core, dsts)
                    g.wait_ge(sem[h + "_w"], front)
                    send(codes(name), dsts, m, s)
                    g.wait_ge(sem[h + "_s"], front)
                    send(plane(name), dsts, m, s)
                if jobs:
                    g.wait_ge(sem["sent"], sent[0])
        return

    _, same, ab, cc = _plan(rank, T, topo)
    own = rank < G
    me = "d%d" % rank
    off, front = masks(rank, core, same, ab)
    arrive = 2 * _count(off)

    if own:
        g.sync.dma_start(codes("a" + me), T.ac[:]).then_inc(sem["ld_a"], 16)
        g.scalar.dma_start(plane("a" + me), T.az[:]).then_inc(sem["ld_a"], 16)
        g.sync.dma_start(codes("b" + me), T.bc[:]).then_inc(sem["ld_b"], 16)
        g.scalar.dma_start(plane("b" + me), T.bs[:]).then_inc(sem["ld_b"], 16)
    g.sync.dma_start(codes("c" + me), T.cc[:]).then_inc(sem["ld_c"], 16)
    g.scalar.dma_start(plane("c" + me), T.cs[:]).then_inc(sem["ld_c"], 16)
    g.scalar.dma_start(T.tx[:], T.x[:]).then_inc(sem["x_in"], 16)

    if own:
        for t in ("a", "b"):
            g.wait_ge(sem["ld_" + t], 32)
            send(codes(t + me), list(ab), front, "h%s_w" % t)
            send(plane(t + me), list(ab), front, "h%s_s" % t)
            send(codes(t + me), same, off, "%s%d" % (t, rank))
            send(plane(t + me), same, off, "%s%d" % (t, rank))
    g.wait_ge(sem["ld_c"], 32)
    send(codes("c" + me), same, off, "c%d" % rank)
    send(plane("c" + me), same, off, "c%d" % rank)
    send(codes("c" + me), list(cc), front, "hc_w")
    send(plane("c" + me), list(cc), front, "hc_s")
    g.wait_ge(sem["sent"], sent[0])

    order = sorted(range(G), key=lambda i: T.cores[i] != core and not topo.may_write(core, T.cores[i]))
    ranks = [(rank + k) % N for k in range(1, N)]
    ranks.sort(key=lambda j: (2 if j < G else 0) + (0 if topo.may_write(core, T.cores[j]) else 1))
    seq = [rank] + ranks

    own_src = {"a": (T.ac, T.az), "b": (T.bc, T.bs), "c": (T.cc, T.cs)}

    def fetch(t, j, part, dst, s):
        if j == rank:
            src = own_src[t][part][:]
        else:
            g.sync.wait_ge(sem["%s%d" % (t, j)], arrive)
            src = (codes, plane)[part]("%sd%d" % (t, j))
        g.sync.dma_start(dst, src).then_inc(sem[s], 16)

    def c_codes(i):
        fetch("c", seq[i], 0, T.c_w[:, cols(i % CW)].bitcast(dt.uint8), "fc%d" % i)

    def c_plane(i):
        fetch("c", seq[i], 1, T.c_s[:, cols(i % CS)], "fp%d" % i)

    i0, i1 = order
    fetch("a", i0, 0, codes("a"), "fa0")
    fetch("a", i0, 1, plane("a"), "fa0")
    c_codes(0)
    c_plane(0)
    g.sync.wait_ge(sem["z%d" % i0], 1)
    fetch("a", i1, 0, codes("a"), "fa1")
    fetch("a", i1, 1, plane("a"), "fa1")
    fetch("b", i0, 0, codes("b"), "fb0")
    fetch("b", i0, 1, T.b_s[:, cols(0)], "fb0")
    fetch("b", i1, 1, T.b_s[:, cols(1)], "fbs")
    g.sync.wait_ge(sem["u%d" % i0], 1)
    fetch("b", i1, 0, codes("b"), "fb1")
    c_codes(1)
    c_plane(1)
    c_plane(2)
    for i in range(CW, N):
        g.sync.wait_ge(sem["mm%d" % (i - CW)], 1)
        c_codes(i)
        if i + 1 < N:
            c_plane(i + 1)

    g.vector.wait_ge(sem["x_in"], 16)
    g.vector.quantize_mx(T.qx_w[:], T.qx_s[:], T.tx[:]).then_inc(sem["qx"], 1)
    for t, z, src, dst, ps in (("a", "z", "x", "g", T.zp), ("b", "u", "g", "h", T.up)):
        tile = T["t" + dst]
        bank = [ps[:, BANK * k:BANK * k + W] for k in range(G)]
        g.tensor.wait_ge(sem["q" + src], 1)
        for k, i in enumerate(order):
            if t == "b" and k:
                g.tensor.wait_ge(sem["fbs"], 16)
                g.tensor.wait_ge(sem["fb1"], 16)
            else:
                g.tensor.wait_ge(sem["f%s%d" % (t, k)], 32)
            lhs = T.a_s[:] if t == "a" else T.b_s[:, cols(k)]
            g.tensor.matmul_mx(bank[k], T[t + "_w"][:], lhs, T["q%s_w" % src][:], T["q%s_s" % src][:],
                               True, True).then_inc(sem["%s%d" % (z, i)], 1)
        rs, rv = sem["rs" + dst], sem["rv" + dst]
        g.scalar.wait_ge(sem["%s%d" % (z, i0)], 1)
        for b, c in ((0, SCALE), (1, -SCALE)):
            g.scalar.activation(tile[:, 2 * i0 + b:4 * W:4], bank[0], ActivationFunctionType.Relu,
                                scale=c).then_inc(rs, 1)
        g.vector.wait_ge(sem["%s%d" % (z, i1)], 1)
        for b, c in ((0, SCALE), (1, -SCALE)):
            g.vector.tensor_scalar(tile[:, 2 * i1 + b:4 * W:4], bank[1], c, 0.0, AluOpType.mult,
                                   AluOpType.max).then_inc(rv, 1)
        g.vector.wait_ge(rs, 2)
        g.vector.wait_ge(rv, 2)
        g.vector.quantize_mx(T["q%s_w" % dst][:], T["q%s_s" % dst][:], tile[:]).then_inc(sem["q" + dst], 1)

    g.tensor.wait_ge(sem["qh"], 1)
    for i in range(N):
        acc = T.yp[:, BANK * (i % 4):BANK * (i % 4) + W]
        stage = T.y_s[:, cols(i % YS)]
        if i >= 4:
            g.tensor.wait_ge(sem["cp%d" % (i - 4)], 1)
        g.tensor.wait_ge(sem["fp%d" % i], 16)
        g.tensor.wait_ge(sem["fc%d" % i], 16)
        g.tensor.matmul_mx(acc, T.c_w[:, cols(i % CW)], T.c_s[:, cols(i % CS)], T.qh_w[:], T.qh_s[:],
                           True, True).then_inc(sem["mm%d" % i], 1)
        g.vector.wait_ge(sem["mm%d" % i], 1)
        if i >= YS:
            g.vector.wait_ge(sem["st%d" % (i - YS)], 16)
        g.vector.tensor_copy(stage, acc).then_inc(sem["cp%d" % i], 1)
        g.scalar.wait_ge(sem["cp%d" % i], 1)
        g.scalar.dma_start(T.y[:, cols(seq[i])], stage).then_inc(sem["st%d" % i], 16)
    for i in range(N - YS, N):
        g.scalar.wait_ge(sem["st%d" % i], 16)
